import numpy as np
import ml_dtypes


def mxq(x, axis, fmt="e4m3"):
    dtype, down = {"e4m3": (ml_dtypes.float8_e4m3fn, 7), "e5m2": (ml_dtypes.float8_e5m2, 14)}[fmt]
    v = np.moveaxis(np.asarray(x, np.float32).astype(ml_dtypes.bfloat16).astype(np.float64), axis, -1)
    blocks = v.reshape(v.shape[:-1] + (-1, 32))
    amax = np.abs(blocks).max(-1, keepdims=True)
    byte = np.maximum(np.where(amax > 0, np.frexp(amax)[1] - 1 + 127, 0) - down, 1)
    scale = np.exp2(byte - 127.0)
    codes = (blocks / scale).astype(np.float32).astype(dtype).astype(np.float64)
    return np.moveaxis((codes * scale).reshape(v.shape), -1, axis)


WIDE = False


def mx_kscale(k):
    if not WIDE:
        return np.ones(k)
    levels = np.array([10, -10, 5, -5, 0])
    if k % 512:
        return np.exp2(np.random.permutation(np.resize(levels, k // 32))).repeat(32)
    a = np.empty((k // 512, 16))
    for p in range(k // 512):
        a[p, :8] = np.random.permutation(np.resize(levels, 8))
        for g in range(8):
            far = levels[np.abs(levels - a[p, g]) >= 10]
            a[p, g + 8] = far[np.random.randint(len(far))]
    return np.exp2(a.ravel()).repeat(32)


def f64(x):
    return np.asarray(x).astype(np.float64)


def striped(idx):
    return np.tile(idx.reshape(-1, 16).T, (8, 1)).astype(np.uint16)


def unstriped(offs):
    return offs[:16].T.reshape(-1).astype(np.int64)


def striped8(idx):
    return np.concatenate([x.reshape(-1, 16).T for x in idx]).astype(np.uint16)


def runs(offs, k):
    lists = np.stack([offs[16 * r : 16 * r + 16].T.reshape(-1) for r in range(8)]).astype(np.int64)
    return lists[np.arange(k) % 512 // 64]


def pack_weight(w):
    k, n = w.shape
    w = f64(np.asarray(w, np.float32).astype(ml_dtypes.bfloat16)).reshape(k // 32, 32, n)
    amax = np.abs(w).max(1)
    byte = np.clip(np.where(amax > 0, np.frexp(amax)[1] - 1 + 127 - 7, 1), 1, 254)
    scaled = (w * np.exp2(127.0 - byte)[:, None, :]).reshape(k, n).astype(np.float32)
    words = np.ascontiguousarray(scaled.reshape(k // 512, 128, 4, n).transpose(0, 1, 3, 2)).astype(ml_dtypes.float8_e4m3fn).view(np.uint8)
    return words, np.ascontiguousarray(byte.astype(np.uint8).reshape(k // 512, 16, n))


def unpack_weight(words, scales):
    g, p, n, _ = words.shape
    vals = np.ascontiguousarray(words).view(ml_dtypes.float8_e4m3fn).astype(np.float64) * np.repeat(np.exp2(scales.astype(np.float64) - 127.0), 8, axis=1)[..., None]
    return vals.transpose(0, 1, 3, 2).reshape(g * 512, n)


def sigmoid(v):
    return 1.0 / (1.0 + np.exp(-np.maximum(v, -700.0)))


K, T, S, N, H = 512, 2048, 256, 512, 512


def setup_inputs():
    n = np.random.standard_normal
    s = mx_kscale(K)[:, None]
    u = mx_kscale(H)
    packed_xT = pack_weight(n((K, T)) * s)
    return {
        "x_words": packed_xT[0],
        "x_scales": packed_xT[1],
        "w1": (n((K, H)) / np.sqrt(K) / s).astype(np.float32),
        "gn": (np.random.uniform(0.5, 1.5, (H, 1)) * u[:, None]).astype(np.float32),
        "w2": (n((H, N)) / np.sqrt(H) / u[:, None]).astype(np.float32),
        "gm": (np.random.uniform(0.5, 1.5, (H, 1)) * u[:, None]).astype(np.float32),
        "w3": (n((H, N)) / np.sqrt(H) / u[:, None]).astype(np.float32),
        "offs": striped(np.random.permutation(T)[:S]),
        "n1": striped(np.random.permutation(S)),
        "n2": striped(np.random.permutation(S)),
        "n3": striped(np.random.permutation(S)),
        "n4": striped8(np.stack([np.random.permutation(S) for _ in range(8)])),
        "n5": striped(np.random.permutation(S)),
        "n6": striped(np.random.permutation(S)),
        "n7": striped(np.random.permutation(S)),
        "n8": striped(np.random.permutation(S)),
    }


def reference(x_words, x_scales, w1, gn, w2, gm, w3, offs, n1, n2, n3, n4, n5, n6, n7, n8):
    xq = unpack_weight(x_words, x_scales)[:, unstriped(offs)]
    y = mxq(f64(w1), 0, "e4m3").T @ xq
    pa = y[:, unstriped(n1)]
    z = f64(gn) * (pa + (sigmoid(y[:, unstriped(n2)])) * (y[:, unstriped(n3)] - pa))
    a = mxq(f64(w2), 0, "e4m3").T @ mxq(z, 0, "e4m3")
    z2 = f64(gm) * (np.maximum(y, y[np.arange(H)[:, None], runs(n4, H)]))
    b = mxq(f64(w3), 0, "e4m3").T @ mxq(z2, 0, "e4m3")
    return np.maximum(a[:, unstriped(n5)] + b[:, unstriped(n7)], a[:, unstriped(n6)] + b[:, unstriped(n8)])

@@ -1,0 +1,198 @@
+from contextlib import ExitStack
+
+import concourse.mybir as mybir
+
+K, T, S, H, N = 512, 2048, 256, 512, 512
+FLOPS = 2 * S * (K * H + 2 * H * N)
+
+F32 = mybir.dt.float32
+BF16 = mybir.dt.bfloat16
+I32 = mybir.dt.int32
+U32 = mybir.dt.uint32
+U16 = mybir.dt.uint16
+U8 = mybir.dt.uint8
+FP8X4 = mybir.dt.float8_e4m3fn_x4
+ALU = mybir.AluOpType
+ACT = mybir.ActivationFunctionType
+
+P = 128
+PACK = 4
+LINE = 4
+Y_WINDOW = 2 * S
+AB_WINDOW = S + 8
+
+
+def tile_picked_forkpathblerpbig_none_p_kernel(
+    tc, x_words, x_scales, w1, gn, w2, gm, w3, offs, n1, n2, n3, n4, n5, n6, n7, n8, out
+):
+    nc = tc.nc
+    with ExitStack() as ctx:
+        sb = ctx.enter_context(tc.tile_pool(name="sb", bufs=1))
+        psum = ctx.enter_context(tc.psum_pool(name="psum", bufs=8))
+
+        def tiles(name, width, dtype=F32):
+            return [sb.tile([P, width], dtype, name="%s%d" % (name, t), align_bytes=64) for t in range(PACK)]
+
+        def load_list(name, source):
+            tile = sb.tile([P, S // 16], U16, name=name)
+            nc.sync.dma_start(tile[:], source)
+            return tile
+
+        def load_rows(name, source, width):
+            tile = sb.tile([P, PACK, width], F32, name=name, align_bytes=64)
+            nc.sync.dma_start(tile[:], source.rearrange("(p j) c -> p j c", j=PACK))
+            return tile
+
+        def interleave(name, planes, width):
+            grouped = sb.tile([P, width, PACK], BF16, name=name, align_bytes=64)
+            nc.vector.tensor_copy(
+                grouped[:].rearrange("p (c i) j -> p c j i", i=LINE),
+                planes[:].rearrange("p j (c i) -> p c j i", i=LINE),
+            )
+            return grouped
+
+        def quantize(name, grouped, width):
+            codes = sb.tile([P, width], U32, name=name + "_codes", align_bytes=64)
+            scales = sb.tile([P, width], U8, name=name + "_scales", align_bytes=64)
+            nc.vector.quantize_mx(
+                out=codes[:].bitcast(FP8X4), scales=scales[:], in_=grouped[:].rearrange("p c j -> p (c j)")
+            )
+            return codes, scales
+
+        def product(weights, moving, t):
+            cols = slice(t * P, (t + 1) * P)
+            acc = psum.tile([P, S], F32, name="acc")
+            nc.tensor.matmul_mx(
+                out=acc[:],
+                lhsT=weights[0][:, cols].bitcast(FP8X4),
+                lhsT_scale=weights[1][:, cols],
+                rhs=moving[0][:].bitcast(FP8X4),
+                rhs_scale=moving[1][:],
+                start=True,
+                stop=True,
+            )
+            return acc
+
+        def fetch(dst, window, offsets, func=ACT.Copy):
+            nc.scalar.activation(dst[:], window[:].indirect(offsets[:]), func)
+
+        scale_table = sb.tile([P, T], U8, name="scale_table", align_bytes=64)
+        nc.vector.memset(scale_table[:].bitcast(I32), 0)
+        for q in range(4):
+            nc.scalar.dma_start(
+                scale_table[32 * q : 32 * q + 4, :].bitcast(I32), x_scales[0, 4 * q : 4 * q + 4, :].bitcast(I32)
+            )
+        w1_raw = sb.tile([P, PACK, H], F32, name="w1_raw", align_bytes=64)
+        w1_rows = w1.rearrange("(p j) c -> p j c", j=PACK)
+        nc.sync.dma_start(w1_raw[:, :2, :], w1_rows[:, :2, :])
+        offs_t = load_list("offs_t", offs)
+        n2_t = load_list("n2_t", n2)
+        n4_t = load_list("n4_t", n4)
+        nc.sync.dma_start(w1_raw[:, 2:, :], w1_rows[:, 2:, :])
+        word_table = sb.tile([P, T], I32, name="word_table", align_bytes=64)
+        nc.sync.dma_start(word_table[:], x_words[0].rearrange("p c r -> p (c r)").bitcast(I32))
+        n1_t = load_list("n1_t", n1)
+        n3_t = load_list("n3_t", n3)
+        w3_raw = load_rows("w3_raw", w3, N)
+        gm_t = load_rows("gm_t", gm, 1)
+        gn_t = load_rows("gn_t", gn, 1)
+        w2_raw = load_rows("w2_raw", w2, N)
+        n7_t = load_list("n7_t", n7)
+        n8_t = load_list("n8_t", n8)
+        n5_t = load_list("n5_t", n5)
+        n6_t = load_list("n6_t", n6)
+
+        y_win = tiles("y_win", Y_WINDOW)
+        a_win = tiles("a_win", AB_WINDOW)
+        b_win = tiles("b_win", AB_WINDOW)
+        for window in y_win + b_win + a_win:
+            nc.vector.memset(window[:, S:], 0.0)
+
+        w1_grouped = sb.tile([P, H, PACK], BF16, name="w1_grouped", align_bytes=64)
+        nc.vector.tensor_copy(
+            w1_grouped[:].rearrange("p (t m) j -> p m j t", t=PACK),
+            w1_raw[:].rearrange("p j (m t) -> p m j t", t=PACK),
+        )
+        x_bytes = sb.tile([P, S], U8, name="x_bytes", align_bytes=64)
+        nc.vector.tensor_copy(x_bytes[:], scale_table[:].indirect(offs_t[:]))
+        w1_q = quantize("w1", w1_grouped, H)
+        x_codes = sb.tile([P, S], U32, name="x_codes", align_bytes=64)
+        nc.vector.tensor_copy(x_codes[:], word_table[:].bitcast(U32).indirect(offs_t[:]))
+        for t in range(PACK):
+            nc.vector.tensor_copy(y_win[t][:, :S], product(w1_q, (x_codes, x_bytes), t)[:])
+
+        y1, gate, y3, y4 = tiles("y1", S), tiles("gate", S), tiles("y3", S), tiles("y4", S)
+        fetch(gate[0], y_win[0], n2_t, ACT.Sigmoid)
+        for t in range(PACK):
+            fetch(y4[t], y_win[t], n4_t)
+        for t in range(PACK):
+            if t > 0:
+                fetch(gate[t], y_win[t], n2_t, ACT.Sigmoid)
+            fetch(y1[t], y_win[t], n1_t)
+            fetch(y3[t], y_win[t], n3_t)
+
+        larger, diff, step = tiles("larger", S), tiles("diff", S), tiles("step", S)
+        z_planes = sb.tile([P, PACK, S], F32, name="z_planes", align_bytes=64)
+        z2_planes = sb.tile([P, PACK, S], F32, name="z2_planes", align_bytes=64)
+
+        def z2_max(t):
+            nc.vector.tensor_tensor(larger[t][:], y4[t][:], y_win[t][:, :S], ALU.max)
+
+        def z2_gain(t):
+            nc.vector.tensor_scalar(z2_planes[:, t, :], larger[t][:], gm_t[:, t, :], None, ALU.mult)
+
+        def z_diff(t):
+            nc.vector.tensor_tensor(diff[t][:], y3[t][:], y1[t][:], ALU.subtract)
+
+        def z_step(t):
+            nc.vector.scalar_tensor_tensor(step[t][:], diff[t][:], gn_t[:, t, :], gate[t][:], ALU.mult, ALU.mult)
+
+        def z_sum(t):
+            nc.vector.scalar_tensor_tensor(z_planes[:, t, :], y1[t][:], gn_t[:, t, :], step[t][:], ALU.mult, ALU.add)
+
+        w3_grouped = interleave("w3_grouped", w3_raw, N)
+        z2_max(0)
+        z2_max(1)
+        w3_q = quantize("w3", w3_grouped, N)
+        z2_max(2)
+        z2_max(3)
+        for t in range(PACK):
+            z2_gain(t)
+        z_diff(0)
+        z2_grouped = interleave("z2_grouped", z2_planes, S)
+        z_step(0)
+        z2_q = quantize("z2", z2_grouped, S)
+        w2_grouped = interleave("w2_grouped", w2_raw, N)
+        b_acc = [product(w3_q, z2_q, t) for t in range(PACK)]
+        z_sum(0)
+        z_diff(1)
+        nc.vector.tensor_copy(b_win[0][:, :S], b_acc[0][:])
+        z_step(1)
+        z_diff(2)
+        z_sum(1)
+        z_step(2)
+        nc.vector.tensor_copy(b_win[1][:, :S], b_acc[1][:])
+        z_sum(2)
+        z_diff(3)
+        w2_q = quantize("w2", w2_grouped, N)
+        z_step(3)
+        nc.vector.tensor_copy(b_win[2][:, :S], b_acc[2][:])
+        z_sum(3)
+        nc.vector.tensor_copy(b_win[3][:, :S], b_acc[3][:])
+        z_grouped = interleave("z_grouped", z_planes, S)
+        z_q = quantize("z", z_grouped, S)
+        for t in range(PACK):
+            nc.vector.tensor_copy(a_win[t][:, :S], product(w2_q, z_q, t)[:])
+
+        a5, a6, b7, b8 = tiles("a5", S), tiles("a6", S), tiles("b7", S), tiles("b8", S)
+        first, second, result = tiles("first", S), tiles("second", S), tiles("result", S)
+        for t in range(PACK):
+            fetch(b7[t], b_win[t], n7_t)
+            fetch(b8[t], b_win[t], n8_t)
+        for t in range(PACK):
+            fetch(a5[t], a_win[t], n5_t)
+            fetch(a6[t], a_win[t], n6_t)
+            nc.vector.tensor_tensor(first[t][:], a5[t][:], b7[t][:], ALU.add)
+            nc.vector.tensor_tensor(second[t][:], a6[t][:], b8[t][:], ALU.add)
+            nc.vector.tensor_tensor(result[t][:], first[t][:], second[t][:], ALU.max)
+            nc.sync.dma_start(out[t * P : (t + 1) * P, :], result[t][:])

@@ -30,8 +30,11 @@ def tile_picked_forkpathblerpbig_none_p_kernel(
         sb = ctx.enter_context(tc.tile_pool(name="sb", bufs=1))
         psum = ctx.enter_context(tc.psum_pool(name="psum", bufs=8))
 
-        def tiles(name, width, dtype=F32):
-            return [sb.tile([P, width], dtype, name="%s%d" % (name, t), align_bytes=64) for t in range(PACK)]
+        def tiles(name, width, tag=None):
+            return [
+                sb.tile([P, width], F32, name="%s%d" % (name, t), tag="%s%d" % (tag or name, t), align_bytes=64)
+                for t in range(PACK)
+            ]
 
         def load_list(name, source):
             tile = sb.tile([P, S // 16], U16, name=name)
@@ -43,8 +46,13 @@ def tile_picked_forkpathblerpbig_none_p_kernel(
             nc.sync.dma_start(tile[:], source.rearrange("(p j) c -> p j c", j=PACK))
             return tile
 
-        def interleave(name, planes, width):
-            grouped = sb.tile([P, width, PACK], BF16, name=name, align_bytes=64)
+        def load_gain(name, source):
+            tile = sb.tile([P, PACK], F32, name=name)
+            nc.sync.dma_start(tile[:], source.rearrange("(p t) o -> p (t o)", t=PACK))
+            return tile
+
+        def interleave(name, planes, width, tag=None):
+            grouped = sb.tile([P, width, PACK], BF16, name=name, tag=tag or name, align_bytes=64)
             nc.vector.tensor_copy(
                 grouped[:].rearrange("p (c i) j -> p c j i", i=LINE),
                 planes[:].rearrange("p j (c i) -> p c j i", i=LINE),
@@ -52,31 +60,31 @@ def tile_picked_forkpathblerpbig_none_p_kernel(
             return grouped
 
         def quantize(name, grouped, width):
-            codes = sb.tile([P, width], U32, name=name + "_codes", align_bytes=64)
+            codes = sb.tile([P, width], U32, name=name + "_codes", tag=name + "_codes", align_bytes=64)
             scales = sb.tile([P, width], U8, name=name + "_scales", align_bytes=64)
             nc.vector.quantize_mx(
                 out=codes[:].bitcast(FP8X4), scales=scales[:], in_=grouped[:].rearrange("p c j -> p (c j)")
             )
             return codes, scales
 
-        def product(weights, moving, t):
+        def product(weights, moving, t, places=slice(0, S)):
             cols = slice(t * P, (t + 1) * P)
-            acc = psum.tile([P, S], F32, name="acc")
+            acc = psum.tile([P, places.stop - places.start], F32, name="acc")
             nc.tensor.matmul_mx(
                 out=acc[:],
                 lhsT=weights[0][:, cols].bitcast(FP8X4),
                 lhsT_scale=weights[1][:, cols],
-                rhs=moving[0][:].bitcast(FP8X4),
-                rhs_scale=moving[1][:],
+                rhs=moving[0][:, places].bitcast(FP8X4),
+                rhs_scale=moving[1][:, places],
                 start=True,
                 stop=True,
             )
             return acc
 
         def fetch(dst, window, offsets, func=ACT.Copy):
-            nc.scalar.activation(dst[:], window[:].indirect(offsets[:]), func)
+            nc.scalar.activation(dst[:, :], window[:].indirect(offsets[:, :]), func)
 
-        scale_table = sb.tile([P, T], U8, name="scale_table", align_bytes=64)
+        scale_table = sb.tile([P, T], U8, name="scale_table", tag="scale_table", align_bytes=64)
         nc.vector.memset(scale_table[:].bitcast(I32), 0)
         for q in range(4):
             nc.scalar.dma_start(
@@ -84,18 +92,18 @@ def tile_picked_forkpathblerpbig_none_p_kernel(
             )
         w1_raw = sb.tile([P, PACK, H], F32, name="w1_raw", align_bytes=64)
         w1_rows = w1.rearrange("(p j) c -> p j c", j=PACK)
-        nc.sync.dma_start(w1_raw[:, :2, :], w1_rows[:, :2, :])
         offs_t = load_list("offs_t", offs)
         n2_t = load_list("n2_t", n2)
-        n4_t = load_list("n4_t", n4)
+        nc.sync.dma_start(w1_raw[:, :2, :], w1_rows[:, :2, :])
         nc.sync.dma_start(w1_raw[:, 2:, :], w1_rows[:, 2:, :])
         word_table = sb.tile([P, T], I32, name="word_table", align_bytes=64)
         nc.sync.dma_start(word_table[:], x_words[0].rearrange("p c r -> p (c r)").bitcast(I32))
+        n4_t = load_list("n4_t", n4)
+        w3_raw = load_rows("w3_raw", w3, N)
         n1_t = load_list("n1_t", n1)
         n3_t = load_list("n3_t", n3)
-        w3_raw = load_rows("w3_raw", w3, N)
-        gm_t = load_rows("gm_t", gm, 1)
-        gn_t = load_rows("gn_t", gn, 1)
+        gm_t = load_gain("gm_t", gm)
+        gn_t = load_gain("gn_t", gn)
         w2_raw = load_rows("w2_raw", w2, N)
         n7_t = load_list("n7_t", n7)
         n8_t = load_list("n8_t", n8)
@@ -109,16 +117,22 @@ def tile_picked_forkpathblerpbig_none_p_kernel(
             nc.vector.memset(window[:, S:], 0.0)
 
         w1_grouped = sb.tile([P, H, PACK], BF16, name="w1_grouped", align_bytes=64)
-        nc.vector.tensor_copy(
-            w1_grouped[:].rearrange("p (t m) j -> p m j t", t=PACK),
-            w1_raw[:].rearrange("p j (m t) -> p m j t", t=PACK),
-        )
+        for rows in (slice(0, 2), slice(2, 4)):
+            nc.vector.tensor_copy(
+                w1_grouped[:, :, rows].rearrange("p (t m) j -> p m j t", t=PACK),
+                w1_raw[:, rows, :].rearrange("p j (m t) -> p m j t", t=PACK),
+            )
         x_bytes = sb.tile([P, S], U8, name="x_bytes", align_bytes=64)
         nc.vector.tensor_copy(x_bytes[:], scale_table[:].indirect(offs_t[:]))
         w1_q = quantize("w1", w1_grouped, H)
-        x_codes = sb.tile([P, S], U32, name="x_codes", align_bytes=64)
-        nc.vector.tensor_copy(x_codes[:], word_table[:].bitcast(U32).indirect(offs_t[:]))
-        for t in range(PACK):
+        x_codes = sb.tile([P, S], U32, name="x_codes", tag="scale_table", align_bytes=64)
+        halves = (slice(0, S // 2), slice(S // 2, S))
+        for places in halves:
+            offsets = offs_t[:, places.start // 16 : places.stop // 16]
+            nc.vector.tensor_copy(x_codes[:, places], word_table[:].bitcast(U32).indirect(offsets))
+        for places in halves:
+            nc.vector.tensor_copy(y_win[0][:, places], product(w1_q, (x_codes, x_bytes), 0, places)[:])
+        for t in range(1, PACK):
             nc.vector.tensor_copy(y_win[t][:, :S], product(w1_q, (x_codes, x_bytes), t)[:])
 
         y1, gate, y3, y4 = tiles("y1", S), tiles("gate", S), tiles("y3", S), tiles("y4", S)
@@ -131,68 +145,80 @@ def tile_picked_forkpathblerpbig_none_p_kernel(
             fetch(y1[t], y_win[t], n1_t)
             fetch(y3[t], y_win[t], n3_t)
 
-        larger, diff, step = tiles("larger", S), tiles("diff", S), tiles("step", S)
+        larger, step = tiles("larger", S), tiles("step", S)
         z_planes = sb.tile([P, PACK, S], F32, name="z_planes", align_bytes=64)
-        z2_planes = sb.tile([P, PACK, S], F32, name="z2_planes", align_bytes=64)
+        z2_planes = sb.tile([P, PACK, S], F32, name="z2_planes", tag="z2_planes", align_bytes=64)
 
         def z2_max(t):
             nc.vector.tensor_tensor(larger[t][:], y4[t][:], y_win[t][:, :S], ALU.max)
 
         def z2_gain(t):
-            nc.vector.tensor_scalar(z2_planes[:, t, :], larger[t][:], gm_t[:, t, :], None, ALU.mult)
+            nc.vector.tensor_scalar(z2_planes[:, t, :], larger[t][:], gm_t[:, t : t + 1], None, ALU.mult)
 
         def z_diff(t):
-            nc.vector.tensor_tensor(diff[t][:], y3[t][:], y1[t][:], ALU.subtract)
+            nc.vector.tensor_tensor(diff[:, t, :], y3[t][:], y1[t][:], ALU.subtract)
 
         def z_step(t):
-            nc.vector.scalar_tensor_tensor(step[t][:], diff[t][:], gn_t[:, t, :], gate[t][:], ALU.mult, ALU.mult)
+            nc.vector.scalar_tensor_tensor(step[t][:], diff[:, t, :], gn_t[:, t : t + 1], gate[t][:], ALU.mult, ALU.mult)
 
         def z_sum(t):
-            nc.vector.scalar_tensor_tensor(z_planes[:, t, :], y1[t][:], gn_t[:, t, :], step[t][:], ALU.mult, ALU.add)
+            nc.vector.scalar_tensor_tensor(z_planes[:, t, :], y1[t][:], gn_t[:, t : t + 1], step[t][:], ALU.mult, ALU.add)
 
-        w3_grouped = interleave("w3_grouped", w3_raw, N)
+        w3_grouped = interleave("w3_grouped", w3_raw, N, tag="w1_codes")
         z2_max(0)
         z2_max(1)
         w3_q = quantize("w3", w3_grouped, N)
         z2_max(2)
+        z2_gain(0)
+        z2_gain(1)
         z2_max(3)
-        for t in range(PACK):
-            z2_gain(t)
-        z_diff(0)
+        z2_gain(2)
+        z2_gain(3)
         z2_grouped = interleave("z2_grouped", z2_planes, S)
-        z_step(0)
+        diff = sb.tile([P, PACK, S], F32, name="diff", tag="z2_planes", align_bytes=64)
+        z_diff(0)
         z2_q = quantize("z2", z2_grouped, S)
-        w2_grouped = interleave("w2_grouped", w2_raw, N)
         b_acc = [product(w3_q, z2_q, t) for t in range(PACK)]
+        w2_grouped = interleave("w2_grouped", w2_raw, N, tag="z2_grouped")
+        z_step(0)
+        w2_q = quantize("w2", w2_grouped, N)
         z_sum(0)
         z_diff(1)
         nc.vector.tensor_copy(b_win[0][:, :S], b_acc[0][:])
         z_step(1)
-        z_diff(2)
-        z_sum(1)
-        z_step(2)
         nc.vector.tensor_copy(b_win[1][:, :S], b_acc[1][:])
-        z_sum(2)
+        z_sum(1)
+        z_diff(2)
+        z_step(2)
         z_diff(3)
-        w2_q = quantize("w2", w2_grouped, N)
+        z_sum(2)
         z_step(3)
         nc.vector.tensor_copy(b_win[2][:, :S], b_acc[2][:])
         z_sum(3)
-        nc.vector.tensor_copy(b_win[3][:, :S], b_acc[3][:])
         z_grouped = interleave("z_grouped", z_planes, S)
+        nc.vector.tensor_copy(b_win[3][:, :S], b_acc[3][:])
         z_q = quantize("z", z_grouped, S)
         for t in range(PACK):
             nc.vector.tensor_copy(a_win[t][:, :S], product(w2_q, z_q, t)[:])
 
-        a5, a6, b7, b8 = tiles("a5", S), tiles("a6", S), tiles("b7", S), tiles("b8", S)
-        first, second, result = tiles("first", S), tiles("second", S), tiles("result", S)
+        a_got, b_got, sums, result = tiles("a_got", 2 * S), tiles("b_got", 2 * S), tiles("sums", 2 * S), tiles("result", S)
         for t in range(PACK):
-            fetch(b7[t], b_win[t], n7_t)
-            fetch(b8[t], b_win[t], n8_t)
-        for t in range(PACK):
-            fetch(a5[t], a_win[t], n5_t)
-            fetch(a6[t], a_win[t], n6_t)
-            nc.vector.tensor_tensor(first[t][:], a5[t][:], b7[t][:], ALU.add)
-            nc.vector.tensor_tensor(second[t][:], a6[t][:], b8[t][:], ALU.add)
-            nc.vector.tensor_tensor(result[t][:], first[t][:], second[t][:], ALU.max)
+            fetch(b_got[t][:, :S], b_win[t], n7_t)
+            fetch(b_got[t][:, S:], b_win[t], n8_t)
+        for t in range(PACK - 1):
+            fetch(a_got[t][:, :S], a_win[t], n5_t)
+            nc.vector.tensor_tensor(sums[t][:, :S], a_got[t][:, :S], b_got[t][:, :S], ALU.add)
+            fetch(a_got[t][:, S:], a_win[t], n6_t)
+            nc.vector.tensor_tensor(sums[t][:, S:], a_got[t][:, S:], b_got[t][:, S:], ALU.add)
+            nc.vector.tensor_tensor(result[t][:], sums[t][:, :S], sums[t][:, S:], ALU.max)
             nc.sync.dma_start(out[t * P : (t + 1) * P, :], result[t][:])
+        t = PACK - 1
+        fetch(a_got[t][:, :S], a_win[t], n5_t)
+        nc.vector.tensor_tensor(sums[t][:, :S], a_got[t][:, :S], b_got[t][:, :S], ALU.add)
+        for half in range(2):
+            cols = slice(half * S // 2, (half + 1) * S // 2)
+            far = slice(S + cols.start, S + cols.stop)
+            fetch(a_got[t][:, far], a_win[t], n6_t[:, cols.start // 16 : cols.stop // 16])
+            nc.vector.tensor_tensor(sums[t][:, far], a_got[t][:, far], b_got[t][:, far], ALU.add)
+            nc.vector.tensor_tensor(result[t][:, cols], sums[t][:, cols], sums[t][:, far], ALU.max)
+            nc.sync.dma_start(out[t * P : (t + 1) * P, cols], result[t][:, cols])

from contextlib import ExitStack

import concourse.mybir as mybir

K, T, S, H, N = 512, 2048, 256, 512, 512
FLOPS = 2 * S * (K * H + 2 * H * N)

F32 = mybir.dt.float32
BF16 = mybir.dt.bfloat16
I32 = mybir.dt.int32
U32 = mybir.dt.uint32
U16 = mybir.dt.uint16
U8 = mybir.dt.uint8
FP8X4 = mybir.dt.float8_e4m3fn_x4
ALU = mybir.AluOpType
ACT = mybir.ActivationFunctionType

P = 128
PACK = 4
LINE = 4
Y_WINDOW = 2 * S
AB_WINDOW = S + 8


def tile_picked_forkpathblerpbig_none_p_kernel(
    tc, x_words, x_scales, w1, gn, w2, gm, w3, offs, n1, n2, n3, n4, n5, n6, n7, n8, out
):
    nc = tc.nc
    with ExitStack() as ctx:
        sb = ctx.enter_context(tc.tile_pool(name="sb", bufs=1))
        psum = ctx.enter_context(tc.psum_pool(name="psum", bufs=8))

        def tiles(name, width, tag=None):
            return [
                sb.tile([P, width], F32, name="%s%d" % (name, t), tag="%s%d" % (tag or name, t), align_bytes=64)
                for t in range(PACK)
            ]

        def load_list(name, source):
            tile = sb.tile([P, S // 16], U16, name=name)
            nc.sync.dma_start(tile[:], source)
            return tile

        def load_rows(name, source, width):
            tile = sb.tile([P, PACK, width], F32, name=name, align_bytes=64)
            nc.sync.dma_start(tile[:], source.rearrange("(p j) c -> p j c", j=PACK))
            return tile

        def load_gain(name, source):
            tile = sb.tile([P, PACK], F32, name=name)
            nc.sync.dma_start(tile[:], source.rearrange("(p t) o -> p (t o)", t=PACK))
            return tile

        def interleave(name, planes, width, tag=None):
            grouped = sb.tile([P, width, PACK], BF16, name=name, tag=tag or name, align_bytes=64)
            nc.vector.tensor_copy(
                grouped[:].rearrange("p (c i) j -> p c j i", i=LINE),
                planes[:].rearrange("p j (c i) -> p c j i", i=LINE),
            )
            return grouped

        def quantize(name, grouped, width):
            codes = sb.tile([P, width], U32, name=name + "_codes", tag=name + "_codes", align_bytes=64)
            scales = sb.tile([P, width], U8, name=name + "_scales", align_bytes=64)
            nc.vector.quantize_mx(
                out=codes[:].bitcast(FP8X4), scales=scales[:], in_=grouped[:].rearrange("p c j -> p (c j)")
            )
            return codes, scales

        def product(weights, moving, t, places=slice(0, S)):
            cols = slice(t * P, (t + 1) * P)
            acc = psum.tile([P, places.stop - places.start], F32, name="acc")
            nc.tensor.matmul_mx(
                out=acc[:],
                lhsT=weights[0][:, cols].bitcast(FP8X4),
                lhsT_scale=weights[1][:, cols],
                rhs=moving[0][:, places].bitcast(FP8X4),
                rhs_scale=moving[1][:, places],
                start=True,
                stop=True,
            )
            return acc

        def fetch(dst, window, offsets, func=ACT.Copy):
            nc.scalar.activation(dst[:, :], window[:].indirect(offsets[:, :]), func)

        scale_table = sb.tile([P, T], U8, name="scale_table", tag="scale_table", align_bytes=64)
        nc.vector.memset(scale_table[:].bitcast(I32), 0)
        for q in range(4):
            nc.scalar.dma_start(
                scale_table[32 * q : 32 * q + 4, :].bitcast(I32), x_scales[0, 4 * q : 4 * q + 4, :].bitcast(I32)
            )
        w1_raw = sb.tile([P, PACK, H], F32, name="w1_raw", align_bytes=64)
        w1_rows = w1.rearrange("(p j) c -> p j c", j=PACK)
        offs_t = load_list("offs_t", offs)
        n2_t = load_list("n2_t", n2)
        nc.sync.dma_start(w1_raw[:, :2, :], w1_rows[:, :2, :])
        nc.sync.dma_start(w1_raw[:, 2:, :], w1_rows[:, 2:, :])
        word_table = sb.tile([P, T], I32, name="word_table", align_bytes=64)
        nc.sync.dma_start(word_table[:], x_words[0].rearrange("p c r -> p (c r)").bitcast(I32))
        n4_t = load_list("n4_t", n4)
        w3_raw = load_rows("w3_raw", w3, N)
        n1_t = load_list("n1_t", n1)
        n3_t = load_list("n3_t", n3)
        gm_t = load_gain("gm_t", gm)
        gn_t = load_gain("gn_t", gn)
        w2_raw = load_rows("w2_raw", w2, N)
        n7_t = load_list("n7_t", n7)
        n8_t = load_list("n8_t", n8)
        n5_t = load_list("n5_t", n5)
        n6_t = load_list("n6_t", n6)

        y_win = tiles("y_win", Y_WINDOW)
        a_win = tiles("a_win", AB_WINDOW)
        b_win = tiles("b_win", AB_WINDOW)
        for window in y_win + b_win + a_win:
            nc.vector.memset(window[:, S:], 0.0)

        w1_grouped = sb.tile([P, H, PACK], BF16, name="w1_grouped", align_bytes=64)
        for rows in (slice(0, 2), slice(2, 4)):
            nc.vector.tensor_copy(
                w1_grouped[:, :, rows].rearrange("p (t m) j -> p m j t", t=PACK),
                w1_raw[:, rows, :].rearrange("p j (m t) -> p m j t", t=PACK),
            )
        x_bytes = sb.tile([P, S], U8, name="x_bytes", align_bytes=64)
        nc.vector.tensor_copy(x_bytes[:], scale_table[:].indirect(offs_t[:]))
        w1_q = quantize("w1", w1_grouped, H)
        x_codes = sb.tile([P, S], U32, name="x_codes", tag="scale_table", align_bytes=64)
        halves = (slice(0, S // 2), slice(S // 2, S))
        for places in halves:
            offsets = offs_t[:, places.start // 16 : places.stop // 16]
            nc.vector.tensor_copy(x_codes[:, places], word_table[:].bitcast(U32).indirect(offsets))
        for places in halves:
            nc.vector.tensor_copy(y_win[0][:, places], product(w1_q, (x_codes, x_bytes), 0, places)[:])
        for t in range(1, PACK):
            nc.vector.tensor_copy(y_win[t][:, :S], product(w1_q, (x_codes, x_bytes), t)[:])

        y1, gate, y3, y4 = tiles("y1", S), tiles("gate", S), tiles("y3", S), tiles("y4", S)
        fetch(gate[0], y_win[0], n2_t, ACT.Sigmoid)
        for t in range(PACK):
            fetch(y4[t], y_win[t], n4_t)
        for t in range(PACK):
            if t > 0:
                fetch(gate[t], y_win[t], n2_t, ACT.Sigmoid)
            fetch(y1[t], y_win[t], n1_t)
            fetch(y3[t], y_win[t], n3_t)

        larger, step = tiles("larger", S), tiles("step", S)
        z_planes = sb.tile([P, PACK, S], F32, name="z_planes", align_bytes=64)
        z2_planes = sb.tile([P, PACK, S], F32, name="z2_planes", tag="z2_planes", align_bytes=64)

        def z2_max(t):
            nc.vector.tensor_tensor(larger[t][:], y4[t][:], y_win[t][:, :S], ALU.max)

        def z2_gain(t):
            nc.vector.tensor_scalar(z2_planes[:, t, :], larger[t][:], gm_t[:, t : t + 1], None, ALU.mult)

        def z_diff(t):
            nc.vector.tensor_tensor(diff[:, t, :], y3[t][:], y1[t][:], ALU.subtract)

        def z_step(t):
            nc.vector.scalar_tensor_tensor(step[t][:], diff[:, t, :], gn_t[:, t : t + 1], gate[t][:], ALU.mult, ALU.mult)

        def z_sum(t):
            nc.vector.scalar_tensor_tensor(z_planes[:, t, :], y1[t][:], gn_t[:, t : t + 1], step[t][:], ALU.mult, ALU.add)

        w3_grouped = interleave("w3_grouped", w3_raw, N, tag="w1_codes")
        z2_max(0)
        z2_max(1)
        w3_q = quantize("w3", w3_grouped, N)
        z2_max(2)
        z2_gain(0)
        z2_gain(1)
        z2_max(3)
        z2_gain(2)
        z2_gain(3)
        z2_grouped = interleave("z2_grouped", z2_planes, S)
        diff = sb.tile([P, PACK, S], F32, name="diff", tag="z2_planes", align_bytes=64)
        z_diff(0)
        z2_q = quantize("z2", z2_grouped, S)
        b_acc = [product(w3_q, z2_q, t) for t in range(PACK)]
        w2_grouped = interleave("w2_grouped", w2_raw, N, tag="z2_grouped")
        z_step(0)
        w2_q = quantize("w2", w2_grouped, N)
        z_sum(0)
        z_diff(1)
        nc.vector.tensor_copy(b_win[0][:, :S], b_acc[0][:])
        z_step(1)
        nc.vector.tensor_copy(b_win[1][:, :S], b_acc[1][:])
        z_sum(1)
        z_diff(2)
        z_step(2)
        z_diff(3)
        z_sum(2)
        z_step(3)
        nc.vector.tensor_copy(b_win[2][:, :S], b_acc[2][:])
        z_sum(3)
        z_grouped = interleave("z_grouped", z_planes, S)
        nc.vector.tensor_copy(b_win[3][:, :S], b_acc[3][:])
        z_q = quantize("z", z_grouped, S)
        for t in range(PACK):
            nc.vector.tensor_copy(a_win[t][:, :S], product(w2_q, z_q, t)[:])

        a_got, b_got, sums, result = tiles("a_got", 2 * S), tiles("b_got", 2 * S), tiles("sums", 2 * S), tiles("result", S)
        for t in range(PACK):
            fetch(b_got[t][:, :S], b_win[t], n7_t)
            fetch(b_got[t][:, S:], b_win[t], n8_t)
        for t in range(PACK - 1):
            fetch(a_got[t][:, :S], a_win[t], n5_t)
            nc.vector.tensor_tensor(sums[t][:, :S], a_got[t][:, :S], b_got[t][:, :S], ALU.add)
            fetch(a_got[t][:, S:], a_win[t], n6_t)
            nc.vector.tensor_tensor(sums[t][:, S:], a_got[t][:, S:], b_got[t][:, S:], ALU.add)
            nc.vector.tensor_tensor(result[t][:], sums[t][:, :S], sums[t][:, S:], ALU.max)
            nc.sync.dma_start(out[t * P : (t + 1) * P, :], result[t][:])
        t = PACK - 1
        fetch(a_got[t][:, :S], a_win[t], n5_t)
        nc.vector.tensor_tensor(sums[t][:, :S], a_got[t][:, :S], b_got[t][:, :S], ALU.add)
        for half in range(2):
            cols = slice(half * S // 2, (half + 1) * S // 2)
            far = slice(S + cols.start, S + cols.stop)
            fetch(a_got[t][:, far], a_win[t], n6_t[:, cols.start // 16 : cols.stop // 16])
            nc.vector.tensor_tensor(sums[t][:, far], a_got[t][:, far], b_got[t][:, far], ALU.add)
            nc.vector.tensor_tensor(result[t][:, cols], sums[t][:, cols], sums[t][:, far], ALU.max)
            nc.sync.dma_start(out[t * P : (t + 1) * P, cols], result[t][:, cols])
